import numpy as np
import ml_dtypes


def mxq(x, axis, fmt="e4m3"):
    dtype, down = {"e4m3": (ml_dtypes.float8_e4m3fn, 7), "e5m2": (ml_dtypes.float8_e5m2, 14)}[fmt]
    v = np.moveaxis(np.asarray(x, np.float32).astype(ml_dtypes.bfloat16).astype(np.float64), axis, -1)
    blocks = v.reshape(v.shape[:-1] + (-1, 32))
    amax = np.abs(blocks).max(-1, keepdims=True)
    byte = np.maximum(np.where(amax > 0, np.frexp(amax)[1] - 1 + 127, 0) - down, 1)
    scale = np.exp2(byte - 127.0)
    codes = (blocks / scale).astype(np.float32).astype(dtype).astype(np.float64)
    return np.moveaxis((codes * scale).reshape(v.shape), -1, axis)


WIDE = False


def mx_kscale(k):
    if not WIDE:
        return np.ones(k)
    levels = np.array([10, -10, 5, -5, 0])
    if k % 512:
        return np.exp2(np.random.permutation(np.resize(levels, k // 32))).repeat(32)
    a = np.empty((k // 512, 16))
    for p in range(k // 512):
        a[p, :8] = np.random.permutation(np.resize(levels, 8))
        for g in range(8):
            far = levels[np.abs(levels - a[p, g]) >= 10]
            a[p, g + 8] = far[np.random.randint(len(far))]
    return np.exp2(a.ravel()).repeat(32)


def f64(x):
    return np.asarray(x).astype(np.float64)


def striped(idx):
    return np.tile(idx.reshape(-1, 16).T, (8, 1)).astype(np.uint16)


def unstriped(offs):
    return offs[:16].T.reshape(-1).astype(np.int64)


def striped8(idx):
    return np.concatenate([x.reshape(-1, 16).T for x in idx]).astype(np.uint16)


def runs(offs, k):
    lists = np.stack([offs[16 * r : 16 * r + 16].T.reshape(-1) for r in range(8)]).astype(np.int64)
    return lists[np.arange(k) % 512 // 64]


def pack_weight(w):
    k, n = w.shape
    w = f64(np.asarray(w, np.float32).astype(ml_dtypes.bfloat16)).reshape(k // 32, 32, n)
    amax = np.abs(w).max(1)
    byte = np.clip(np.where(amax > 0, np.frexp(amax)[1] - 1 + 127 - 7, 1), 1, 254)
    scaled = (w * np.exp2(127.0 - byte)[:, None, :]).reshape(k, n).astype(np.float32)
    words = np.ascontiguousarray(scaled.reshape(k // 512, 128, 4, n).transpose(0, 1, 3, 2)).astype(ml_dtypes.float8_e4m3fn).view(np.uint8)
    return words, np.ascontiguousarray(byte.astype(np.uint8).reshape(k // 512, 16, n))


def unpack_weight(words, scales):
    g, p, n, _ = words.shape
    vals = np.ascontiguousarray(words).view(ml_dtypes.float8_e4m3fn).astype(np.float64) * np.repeat(np.exp2(scales.astype(np.float64) - 127.0), 8, axis=1)[..., None]
    return vals.transpose(0, 1, 3, 2).reshape(g * 512, n)

def planes(y):
    n, m = y.shape
    v = y.astype(np.float32).astype(ml_dtypes.bfloat16).astype(np.float64).reshape(n // 32, 32, m)
    top = np.abs(v).max(1)
    byte = np.clip(np.where(top > 0, np.frexp(top)[1] - 1 + 127 - 7, 1), 1, 254)
    codes = (v * np.exp2(127.0 - byte)[:, None, :]).reshape(n, m).astype(np.float32).astype(ml_dtypes.float8_e4m3fn).view(np.uint8)
    words = codes.reshape(n // 512, 128, 4, m).transpose(0, 1, 3, 2)
    return np.ascontiguousarray(words), np.ascontiguousarray(byte.astype(np.uint8).reshape(n // 512, 16, m))


K, T, S, N, H = 512, 2048, 512, 512, 512


def setup_inputs():
    n = np.random.standard_normal
    s = mx_kscale(K)[:, None]
    u = mx_kscale(H)
    packed_xT = pack_weight(n((K, T)) * s)
    packed_w1 = pack_weight(n((K, H)) / np.sqrt(K) / s)
    packed_w2 = pack_weight(n((K, H)) / np.sqrt(K) / s)
    packed_w3 = pack_weight(n((H, N)) / np.sqrt(H) / u[:, None])
    return {
        "x_words": packed_xT[0],
        "x_scales": packed_xT[1],
        "w1_words": packed_w1[0],
        "w1_scales": packed_w1[1],
        "w2_words": packed_w2[0],
        "w2_scales": packed_w2[1],
        "tau": np.random.uniform(0.3, 0.9, (H, 1)).astype(np.float32),
        "gn": (np.random.uniform(0.5, 1.5, (H, 1)) * u[:, None]).astype(np.float32),
        "w3_words": packed_w3[0],
        "w3_scales": packed_w3[1],
        "tau2": np.random.uniform(0.2, 0.6, (N, 1)).astype(np.float32),
        "tau3": np.random.uniform(0.6, 1.0, (N, 1)).astype(np.float32),
        "offs": striped(np.random.permutation(T)[:S]),
        "two": striped(np.random.permutation(T)[:S]),
        "n1": striped(np.random.permutation(S)),
        "n2": striped(np.random.permutation(S)),
        "n3": striped8(np.stack([np.random.permutation(S) for _ in range(8)])),
        "n4": striped8(np.stack([np.random.permutation(S) for _ in range(8)])),
    }


def reference(x_words, x_scales, w1_words, w1_scales, w2_words, w2_scales, tau, gn, w3_words, w3_scales, tau2, tau3, offs, two, n1, n2, n3, n4):
    x_two = unpack_weight(x_words, x_scales)[:, unstriped(two)]
    d = unpack_weight(w2_words, w2_scales).T @ x_two
    top = d.max(axis=1, keepdims=True)
    ea = np.exp(f64(tau) * (d[:, unstriped(n1)] - top))
    xq = unpack_weight(x_words, x_scales)[:, unstriped(offs)]
    y = unpack_weight(w1_words, w1_scales).T @ xq
    z = f64(gn) * ((2.0 * ea) * (y - y[:, unstriped(n2)]) - (0.5 * d))
    h = unpack_weight(w3_words, w3_scales).T @ mxq(z, 0, "e4m3")
    top2 = h.max(axis=1, keepdims=True)
    ea2 = np.exp(f64(tau2) * (h[np.arange(N)[:, None], runs(n3, N)] - top2))
    ea3 = np.exp(f64(tau3) * (h[np.arange(N)[:, None], runs(n4, N)] - top2))
    out_0 = 3.0 * (ea2 - ea3)
    return (out_0,) + planes(out_0)

@@ -1,0 +1,235 @@
+from contextlib import ExitStack
+
+import concourse.mybir as mybir
+
+K, T, S, N, H = 512, 2048, 512, 512, 512
+FLOPS = 3 * 2 * 512 * 512 * 512
+
+F32 = mybir.dt.float32
+BF16 = mybir.dt.bfloat16
+U32 = mybir.dt.uint32
+I32 = mybir.dt.int32
+U16 = mybir.dt.uint16
+U8 = mybir.dt.uint8
+FP8X4 = mybir.dt.float8_e4m3fn_x4
+ALU = mybir.AluOpType
+ACT = mybir.ActivationFunctionType
+
+P = 128
+Z_PIECES = ((0, 256), (256, 512))
+OUT_PIECES = ((0, 256), (256, 384), (384, 512))
+
+
+def words_of(dram):
+    return dram[0].rearrange("p n t -> p (n t)").bitcast(I32)
+
+
+def load_scale_rows(queue, tile, dram, quadrants):
+    for q in quadrants:
+        queue.dma_start(
+            out=tile[32 * q : 32 * q + 4, :].bitcast(I32),
+            in_=dram[0, 4 * q : 4 * q + 4, :].bitcast(I32),
+        )
+
+
+def offsets(lst, a, b):
+    return lst[:, a // 16 : b // 16]
+
+
+def woven(ap):
+    return ap.rearrange("p (c i t) -> p c t i", i=4, t=4)
+
+
+def by_fours(ap):
+    return ap.rearrange("p t (c i) -> p c t i", i=4)
+
+
+def tile_picked_twlpxbetw_none_po_kernel(
+    tc, x_words, x_scales, w1_words, w1_scales, w2_words, w2_scales, tau, gn, w3_words, w3_scales,
+    tau2, tau3, offs, two, n1, n2, n3, n4, out_0, out_1, out_2,
+):
+    nc = tc.nc
+    with ExitStack() as ctx:
+        keep = ctx.enter_context(tc.tile_pool(name="keep", bufs=1))
+        psum = ctx.enter_context(tc.psum_pool(name="psum", bufs=1))
+
+        def sb(name, shape, dt, tag=None):
+            return keep.tile(shape, dt, name=name, tag=tag or name, align_bytes=64)
+
+        lists = {nm: keep.tile([P, S // 16], U16, name="list_" + nm) for nm in ("offs", "two", "n1", "n2", "n3", "n4")}
+        xw = sb("xw", [P, T], U32)
+        xs = sb("xs", [P, T], U8)
+        raw_w = [sb("raw_w%d" % i, [P, 512], U32) for i in range(3)]
+        dealt_w = [sb("dealt_w%d" % i, [P, 512], U32) for i in range(3)]
+        raw_s = [sb("raw_s%d" % i, [P, 512], U8) for i in range(3)]
+        dealt_s = [sb("dealt_s%d" % i, [P, 512], U8) for i in range(3)]
+        vec = {nm: sb("vec_" + nm, [P, 4], F32) for nm in ("tau", "gn", "tau2", "tau3")}
+
+        nc.vector.memset(xs[:].bitcast(I32), 0)
+        for i in range(3):
+            nc.gpsimd.memset(raw_s[i][:].bitcast(I32), 0)
+
+        def load_vec(queue, name, dram):
+            queue.dma_start(out=vec[name][:], in_=dram.rearrange("(p t) o -> p (t o)", t=4))
+
+        load_vec(nc.scalar, "tau", tau)
+        load_scale_rows(nc.scalar, raw_s[0], w1_scales, (0,))
+        nc.scalar.dma_start(out=xw[:].bitcast(I32), in_=words_of(x_words))
+        nc.scalar.dma_start(out=raw_w[0][:].bitcast(I32), in_=words_of(w1_words))
+        neg_tau = sb("neg_tau", [P, 4], F32)
+        nc.scalar.activation(neg_tau[:], vec["tau"][:], ACT.Copy, scale=-1.0)
+        nc.scalar.dma_start(out=raw_w[1][:].bitcast(I32), in_=words_of(w2_words))
+        load_scale_rows(nc.gpsimd, raw_s[0], w1_scales, (2, 3))
+        load_vec(nc.gpsimd, "gn", gn)
+        load_vec(nc.gpsimd, "tau2", tau2)
+        load_vec(nc.gpsimd, "tau3", tau3)
+        nc.sync.dma_start(lists["offs"][:], offs)
+        load_scale_rows(nc.sync, xs, x_scales, range(4))
+        load_scale_rows(nc.sync, raw_s[0], w1_scales, (1,))
+        nc.sync.dma_start(lists["n2"][:], n2)
+        nc.sync.dma_start(lists["two"][:], two)
+        load_scale_rows(nc.sync, raw_s[1], w2_scales, range(4))
+        nc.sync.dma_start(lists["n1"][:], n1)
+        load_scale_rows(nc.sync, raw_s[2], w3_scales, range(4))
+        nc.sync.dma_start(out=raw_w[2][:].bitcast(I32), in_=words_of(w3_words))
+        nc.sync.dma_start(lists["n3"][:], n3)
+        nc.sync.dma_start(lists["n4"][:], n4)
+
+        def deal_words(engine_copy, i):
+            engine_copy(
+                out=dealt_w[i][:].rearrange("p (t m) -> p m t", t=4),
+                in_=raw_w[i][:].rearrange("p (m t) -> p m t", t=4),
+            )
+
+        def deal_bytes(engine_copy, i):
+            engine_copy(
+                out=dealt_s[i][:].rearrange("p (t m) -> p t m", t=4),
+                in_=raw_s[i][:].rearrange("p (m t) -> p t m", t=4),
+            )
+
+        def pick(name):
+            words = sb("picked_w_" + name, [P, S], U32)
+            scales = sb("picked_s_" + name, [P, S], U8)
+            nc.vector.tensor_copy(scales[:], xs[:].indirect(lists[name][:]))
+            nc.vector.tensor_copy(words[:], xw[:].indirect(lists[name][:]))
+            return words, scales
+
+        def product(bank, i, t, words, scales):
+            cols = slice(128 * t, 128 * (t + 1))
+            nc.tensor.matmul_mx(
+                out=bank, lhsT=dealt_w[i][:, cols].bitcast(FP8X4), lhsT_scale=dealt_s[i][:, cols],
+                rhs=words.bitcast(FP8X4), rhs_scale=scales, start=True, stop=True,
+            )
+
+        deal_bytes(nc.vector.tensor_copy, 0)
+        deal_words(nc.scalar.copy, 0)
+        xq_w, xq_s = pick("offs")
+        y_bank = [psum.tile([P, S], F32, name="y_bank%d" % t, tag="a%d" % t) for t in range(4)]
+        for t in range(4):
+            product(y_bank[t][:], 0, t, xq_w[:], xq_s[:])
+        deal_bytes(nc.gpsimd.tensor_copy, 1)
+        deal_words(nc.gpsimd.tensor_copy, 1)
+        x2_w, x2_s = pick("two")
+        d_bank = [psum.tile([P, S], F32, name="d_bank%d" % t, tag="b%d" % t) for t in range(4)]
+        for t in range(4):
+            product(d_bank[t][:], 1, t, x2_w[:], x2_s[:])
+
+        gn_twice = sb("gn_twice", [P, 4], F32)
+        gn_half = sb("gn_half", [P, 4], F32)
+        neg_tau23 = sb("neg_tau23", [P, 4, 2], F32)
+        nc.gpsimd.tensor_scalar(gn_twice[:], vec["gn"][:], 2.0, 0.0, ALU.mult, ALU.add)
+        nc.gpsimd.tensor_scalar(gn_half[:], vec["gn"][:], -0.5, 0.0, ALU.mult, ALU.add)
+
+        y_sb = [sb("y_sb%d" % t, [P, S], F32) for t in range(4)]
+        d_sb = [sb("d_sb%d" % t, [P, S], F32) for t in range(4)]
+        top = [sb("top%d" % t, [P, 1], F32) for t in range(3)]
+        top.append(keep.tile([P, 1], F32, name="top3", tag="late", align_bytes=64))
+        bias = [sb("bias%d" % t, [P, 1], F32) for t in range(4)]
+        d_half = sb("d_half", [P, 4, S], F32)
+
+        for t in range(4):
+            nc.vector.tensor_scalar(d_sb[t][:], d_bank[t][:], 1.0, None, ALU.mult, ALU.max, accum_out=top[t][:])
+        for t in range(4):
+            nc.vector.tensor_scalar(bias[t][:], top[t][:], neg_tau[:, t : t + 1], None, ALU.mult)
+            nc.gpsimd.tensor_scalar(d_half[:, t, :], d_sb[t][:], gn_half[:, t : t + 1], 0.0, ALU.mult, ALU.add)
+        deal_bytes(nc.gpsimd.tensor_copy, 2)
+        deal_words(nc.gpsimd.tensor_copy, 2)
+        nc.gpsimd.tensor_scalar(neg_tau23[:, :, 0], vec["tau2"][:], -1.0, 0.0, ALU.mult, ALU.add)
+        nc.gpsimd.tensor_scalar(neg_tau23[:, :, 1], vec["tau3"][:], -1.0, 0.0, ALU.mult, ALU.add)
+
+        z_w, z_s = [], []
+        for k, (a, b) in enumerate(Z_PIECES):
+            n = b - a
+            if k == 0:
+                y_got = sb("y_got0", [P, 4, n], F32)
+            else:
+                y_got = keep.tile([P, 4, n], F32, name="y_got%d" % k, tag="late", align_bytes=64)
+            gap = sb("gap%d" % k, [P, 4, n], F32)
+            ea = sb("ea%d" % k, [P, 4, n], F32)
+            pull = sb("pull%d" % k, [P, 4, n], F32, "pull")
+            z = sb("z%d" % k, [P, 4 * n], BF16, "z")
+            z_w.append(sb("z_w%d" % k, [P, n], U32))
+            z_s.append(sb("z_s%d" % k, [P, n], U8))
+            for t in range(4):
+                if k == 0:
+                    nc.scalar.copy(y_sb[t][:], y_bank[t][:])
+                nc.scalar.activation(y_got[:, t, :], y_sb[t][:].indirect(offsets(lists["n2"], a, b)), ACT.Copy)
+                nc.vector.tensor_tensor(gap[:, t, :], y_bank[t][:, a:b], y_got[:, t, :], ALU.subtract)
+            for t in range(4):
+                nc.scalar.activation(
+                    ea[:, t, :], d_sb[t][:].indirect(offsets(lists["n1"], a, b)), ACT.Exp,
+                    bias=bias[t][:], scale=vec["tau"][:, t : t + 1],
+                )
+                nc.vector.scalar_tensor_tensor(
+                    pull[:, t, :], gap[:, t, :], gn_twice[:, t : t + 1], ea[:, t, :], ALU.mult, ALU.mult
+                )
+            nc.vector.tensor_tensor(woven(z[:]), by_fours(pull[:]), by_fours(d_half[:, :, a:b]), ALU.add)
+            nc.vector.quantize_mx(out=z_w[k][:].bitcast(FP8X4), scales=z_s[k][:], in_=z[:])
+
+        h_sb = [sb("h_sb%d" % t, [P, S], F32) for t in range(4)]
+        top2 = [[sb("top2_%d_%d" % (k, t), [P, 1], F32) for t in range(4)] for k in range(len(Z_PIECES))]
+        bias23 = [sb("bias23_%d" % t, [P, 2], F32) for t in range(4)]
+        h_bank = []
+        for k, (a, b) in enumerate(Z_PIECES):
+            h_bank.append([psum.tile([P, S], F32, name="h_bank%d_%d" % (k, t), tag="%s%d" % ("ba"[k], t)) for t in range(4)])
+            for t in range(4):
+                product(h_bank[k][t][:, 0 : b - a], 2, t, z_w[k][:], z_s[k][:])
+        for t in range(4):
+            for k, (a, b) in enumerate(Z_PIECES):
+                before = top2[k - 1][t][:] if k else None
+                nc.vector.tensor_scalar(
+                    h_sb[t][:, a:b], h_bank[k][t][:, 0 : b - a], 1.0, before, ALU.mult, ALU.max,
+                    accum_out=top2[k][t][:],
+                )
+            nc.vector.tensor_scalar(bias23[t][:], neg_tau23[:, t, :], top2[-1][t][:], None, ALU.mult)
+
+        out_w = sb("out_w", [P, S], U32)
+        out_s = sb("out_s", [P, S], U8)
+        rows = out_0.rearrange("(p t) j -> p t j", t=4)
+        for k, (a, b) in enumerate(OUT_PIECES):
+            n = b - a
+            ea2 = sb("ea2_%d" % k, [P, 4, n], F32)
+            ea3 = sb("ea3_%d" % k, [P, 4, n], F32)
+            diff = sb("diff%d" % k, [P, 4, n], F32)
+            res = sb("res%d" % k, [P, 4, n], F32)
+            rounded = sb("rounded%d" % k, [P, 4 * n], BF16, "rounded")
+            for t in range(4):
+                for got, lst, rate, col in ((ea2, "n3", "tau2", 0), (ea3, "n4", "tau3", 1)):
+                    nc.scalar.activation(
+                        got[:, t, :], h_sb[t][:].indirect(offsets(lists[lst], a, b)), ACT.Exp,
+                        bias=bias23[t][:, col : col + 1], scale=vec[rate][:, t : t + 1],
+                    )
+                nc.vector.tensor_tensor(diff[:, t, :], ea2[:, t, :], ea3[:, t, :], ALU.subtract)
+            nc.vector.tensor_scalar(woven(rounded[:]), by_fours(diff[:]), 3.0, None, ALU.mult)
+            if k == len(OUT_PIECES) - 1:
+                nc.scalar.activation(res[:], diff[:], ACT.Copy, scale=3.0)
+            else:
+                nc.vector.tensor_scalar(res[:], diff[:], 3.0, None, ALU.mult)
+            nc.vector.quantize_mx(out=out_w[:, a:b].bitcast(FP8X4), scales=out_s[:, a:b], in_=rounded[:])
+            nc.sync.dma_start(out=rows[:, :, a:b], in_=res[:])
+            nc.sync.dma_start(out=words_of(out_1)[:, a:b], in_=out_w[:, a:b].bitcast(I32))
+        for q in range(4):
+            queue = nc.scalar if q % 2 else nc.sync
+            queue.dma_start(
+                out=out_2[0, 4 * q : 4 * q + 4, :].bitcast(I32), in_=out_s[32 * q : 32 * q + 4, :].bitcast(I32)
+            )

@@ -18,10 +18,19 @@ ACT = mybir.ActivationFunctionType
 P = 128
 Z_PIECES = ((0, 256), (256, 512))
 OUT_PIECES = ((0, 256), (256, 384), (384, 512))
+Y_ON_VECTOR = (2,)
+SPLIT_H = (0, 1)
+BIAS_ON_SCALAR = (0,)
+SPARE = 16
+HALF_ON_SCALAR = ()
 
 
 def words_of(dram):
     return dram[0].rearrange("p n t -> p (n t)").bitcast(I32)
+
+
+def by_rows(column):
+    return column.rearrange("(p t) o -> p (t o)", t=4)
 
 
 def load_scale_rows(queue, tile, dram, quadrants):
@@ -59,41 +68,44 @@ def tile_picked_twlpxbetw_none_po_kernel(
         lists = {nm: keep.tile([P, S // 16], U16, name="list_" + nm) for nm in ("offs", "two", "n1", "n2", "n3", "n4")}
         xw = sb("xw", [P, T], U32)
         xs = sb("xs", [P, T], U8)
-        raw_w = [sb("raw_w%d" % i, [P, 512], U32) for i in range(3)]
-        dealt_w = [sb("dealt_w%d" % i, [P, 512], U32) for i in range(3)]
-        raw_s = [sb("raw_s%d" % i, [P, 512], U8) for i in range(3)]
-        dealt_s = [sb("dealt_s%d" % i, [P, 512], U8) for i in range(3)]
-        vec = {nm: sb("vec_" + nm, [P, 4], F32) for nm in ("tau", "gn", "tau2", "tau3")}
+        raw_w = {i: sb("raw_w%d" % i, [P, 512], U32) for i in (1, 2, 3)}
+        dealt_w = {i: sb("dealt_w%d" % i, [P, 512], U32) for i in (1, 2, 3)}
+        raw_s = {i: sb("raw_s%d" % i, [P, 512], U8) for i in (1, 2, 3)}
+        dealt_s = {i: sb("dealt_s%d" % i, [P, 512], U8) for i in (1, 2, 3)}
+        rate = sb("rate", [P, 4], F32)
+        gain = sb("gain", [P, 4], F32)
+        neg_rate = sb("neg_rate", [P, 4], F32)
+        rate23 = sb("rate23", [P, 2, 8], F32)
 
-        nc.vector.memset(xs[:].bitcast(I32), 0)
-        for i in range(3):
-            nc.gpsimd.memset(raw_s[i][:].bitcast(I32), 0)
-
-        def load_vec(queue, name, dram):
-            queue.dma_start(out=vec[name][:], in_=dram.rearrange("(p t) o -> p (t o)", t=4))
-
-        load_vec(nc.scalar, "tau", tau)
-        load_scale_rows(nc.scalar, raw_s[0], w1_scales, (0,))
+        nc.vector.memset(xs[:, 0 : T // 2].bitcast(I32), 0)
+        nc.gpsimd.memset(xs[:, T // 2 : T].bitcast(I32), 0)
+        for i in (1, 2, 3):
+            nc.vector.memset(raw_s[i][:].bitcast(I32), 0)
+        y_sb = [sb("y_sb%d" % t, [P, S + SPARE], F32) for t in range(4)]
+        for t in range(4):
+            nc.vector.memset(y_sb[t][:, S:], 0.0)
+        nc.scalar.dma_start(out=rate[:], in_=by_rows(tau))
+        load_scale_rows(nc.scalar, xs, x_scales, (0, 2))
         nc.scalar.dma_start(out=xw[:].bitcast(I32), in_=words_of(x_words))
-        nc.scalar.dma_start(out=raw_w[0][:].bitcast(I32), in_=words_of(w1_words))
-        neg_tau = sb("neg_tau", [P, 4], F32)
-        nc.scalar.activation(neg_tau[:], vec["tau"][:], ACT.Copy, scale=-1.0)
-        nc.scalar.dma_start(out=raw_w[1][:].bitcast(I32), in_=words_of(w2_words))
-        load_scale_rows(nc.gpsimd, raw_s[0], w1_scales, (2, 3))
-        load_vec(nc.gpsimd, "gn", gn)
-        load_vec(nc.gpsimd, "tau2", tau2)
-        load_vec(nc.gpsimd, "tau3", tau3)
+        nc.scalar.dma_start(out=raw_w[1][:].bitcast(I32), in_=words_of(w1_words))
+        nc.scalar.dma_start(out=raw_w[2][:].bitcast(I32), in_=words_of(w2_words))
+        nc.scalar.activation(neg_rate[:], rate[:], ACT.Copy, scale=-1.0)
         nc.sync.dma_start(lists["offs"][:], offs)
-        load_scale_rows(nc.sync, xs, x_scales, range(4))
-        load_scale_rows(nc.sync, raw_s[0], w1_scales, (1,))
-        nc.sync.dma_start(lists["n2"][:], n2)
         nc.sync.dma_start(lists["two"][:], two)
-        load_scale_rows(nc.sync, raw_s[1], w2_scales, range(4))
+        load_scale_rows(nc.sync, xs, x_scales, (1, 3))
+        load_scale_rows(nc.sync, raw_s[1], w1_scales, (0, 1, 2))
+        load_scale_rows(nc.sync, raw_s[2], w2_scales, (0, 1, 2))
+        nc.sync.dma_start(lists["n2"][:], n2)
         nc.sync.dma_start(lists["n1"][:], n1)
-        load_scale_rows(nc.sync, raw_s[2], w3_scales, range(4))
-        nc.sync.dma_start(out=raw_w[2][:].bitcast(I32), in_=words_of(w3_words))
+        load_scale_rows(nc.sync, raw_s[3], w3_scales, range(4))
         nc.sync.dma_start(lists["n3"][:], n3)
         nc.sync.dma_start(lists["n4"][:], n4)
+        for j, column in enumerate((tau2, tau3)):
+            nc.sync.dma_start(out=rate23[:, j, 0:4], in_=by_rows(column))
+        nc.gpsimd.dma_start(out=gain[:], in_=by_rows(gn))
+        load_scale_rows(nc.gpsimd, raw_s[1], w1_scales, (3,))
+        load_scale_rows(nc.gpsimd, raw_s[2], w2_scales, (3,))
+        nc.gpsimd.dma_start(out=raw_w[3][:].bitcast(I32), in_=words_of(w3_words))
 
         def deal_words(engine_copy, i):
             engine_copy(
@@ -101,18 +113,11 @@ def tile_picked_twlpxbetw_none_po_kernel(
                 in_=raw_w[i][:].rearrange("p (m t) -> p m t", t=4),
             )
 
-        def deal_bytes(engine_copy, i):
-            engine_copy(
+        def deal_bytes(i):
+            (nc.gpsimd if i == 3 else nc.vector).tensor_copy(
                 out=dealt_s[i][:].rearrange("p (t m) -> p t m", t=4),
                 in_=raw_s[i][:].rearrange("p (m t) -> p t m", t=4),
             )
-
-        def pick(name):
-            words = sb("picked_w_" + name, [P, S], U32)
-            scales = sb("picked_s_" + name, [P, S], U8)
-            nc.vector.tensor_copy(scales[:], xs[:].indirect(lists[name][:]))
-            nc.vector.tensor_copy(words[:], xw[:].indirect(lists[name][:]))
-            return words, scales
 
         def product(bank, i, t, words, scales):
             cols = slice(128 * t, 128 * (t + 1))
@@ -121,87 +126,116 @@ def tile_picked_twlpxbetw_none_po_kernel(
                 rhs=words.bitcast(FP8X4), rhs_scale=scales, start=True, stop=True,
             )
 
-        deal_bytes(nc.vector.tensor_copy, 0)
-        deal_words(nc.scalar.copy, 0)
-        xq_w, xq_s = pick("offs")
-        y_bank = [psum.tile([P, S], F32, name="y_bank%d" % t, tag="a%d" % t) for t in range(4)]
-        for t in range(4):
-            product(y_bank[t][:], 0, t, xq_w[:], xq_s[:])
-        deal_bytes(nc.gpsimd.tensor_copy, 1)
-        deal_words(nc.gpsimd.tensor_copy, 1)
-        x2_w, x2_s = pick("two")
+        picked_w = {nm: sb("picked_w_" + nm, [P, S], U32) for nm in ("two", "offs")}
+        picked_s = {nm: sb("picked_s_" + nm, [P, S], U8) for nm in ("two", "offs")}
+        for nm in ("offs", "two"):
+            nc.vector.tensor_copy(picked_s[nm][:], xs[:].indirect(lists[nm][:]))
+        deal_bytes(1)
+        for i in (1, 2, 3):
+            deal_words(nc.scalar.copy, i)
+        for nm in ("offs", "two"):
+            nc.vector.tensor_copy(picked_w[nm][:], xw[:].indirect(lists[nm][:]))
+        deal_bytes(2)
         d_bank = [psum.tile([P, S], F32, name="d_bank%d" % t, tag="b%d" % t) for t in range(4)]
-        for t in range(4):
-            product(d_bank[t][:], 1, t, x2_w[:], x2_s[:])
+        y_bank = [psum.tile([P, S], F32, name="y_bank%d" % t, tag="a%d" % t) for t in range(4)]
+        for step in "y0 y1 d0 y2 d1 y3 d2 d3".split():
+            t = int(step[1])
+            if step[0] == "y":
+                product(y_bank[t][:], 1, t, picked_w["offs"][:], picked_s["offs"][:])
+            else:
+                product(d_bank[t][:], 2, t, picked_w["two"][:], picked_s["two"][:])
 
-        gn_twice = sb("gn_twice", [P, 4], F32)
-        gn_half = sb("gn_half", [P, 4], F32)
-        neg_tau23 = sb("neg_tau23", [P, 4, 2], F32)
-        nc.gpsimd.tensor_scalar(gn_twice[:], vec["gn"][:], 2.0, 0.0, ALU.mult, ALU.add)
-        nc.gpsimd.tensor_scalar(gn_half[:], vec["gn"][:], -0.5, 0.0, ALU.mult, ALU.add)
 
-        y_sb = [sb("y_sb%d" % t, [P, S], F32) for t in range(4)]
         d_sb = [sb("d_sb%d" % t, [P, S], F32) for t in range(4)]
-        top = [sb("top%d" % t, [P, 1], F32) for t in range(3)]
-        top.append(keep.tile([P, 1], F32, name="top3", tag="late", align_bytes=64))
+        top = [sb("top%d" % t, [P, 1], F32) for t in range(4)]
         bias = [sb("bias%d" % t, [P, 1], F32) for t in range(4)]
         d_half = sb("d_half", [P, 4, S], F32)
+        half_gain = sb("half_gain", [P, 4], F32)
 
+        for t in Y_ON_VECTOR:
+            nc.vector.tensor_scalar(y_sb[t][:, 0:S], y_bank[t][:], 2.0, None, ALU.mult)
         for t in range(4):
             nc.vector.tensor_scalar(d_sb[t][:], d_bank[t][:], 1.0, None, ALU.mult, ALU.max, accum_out=top[t][:])
-        for t in range(4):
-            nc.vector.tensor_scalar(bias[t][:], top[t][:], neg_tau[:, t : t + 1], None, ALU.mult)
-            nc.gpsimd.tensor_scalar(d_half[:, t, :], d_sb[t][:], gn_half[:, t : t + 1], 0.0, ALU.mult, ALU.add)
-        deal_bytes(nc.gpsimd.tensor_copy, 2)
-        deal_words(nc.gpsimd.tensor_copy, 2)
-        nc.gpsimd.tensor_scalar(neg_tau23[:, :, 0], vec["tau2"][:], -1.0, 0.0, ALU.mult, ALU.add)
-        nc.gpsimd.tensor_scalar(neg_tau23[:, :, 1], vec["tau3"][:], -1.0, 0.0, ALU.mult, ALU.add)
+            nc.vector.tensor_scalar(bias[t][:], top[t][:], neg_rate[:, t : t + 1], None, ALU.mult)
+        if HALF_ON_SCALAR:
+            nc.vector.tensor_scalar(half_gain[:], gain[:], -0.5, None, ALU.mult)
+
+        HALVES = ((0, 256), (256, 512))
+        ea = sb("ea", [P, 4, S], F32)
+        y_got = sb("y_got", [P, 4, S], F32)
+        gap = sb("gap", [P, 4, S], F32)
+
+        def fetch_ea(a, b):
+            for t in range(4):
+                nc.scalar.activation(
+                    ea[:, t, a:b], d_sb[t][:].indirect(offsets(lists["n1"], a, b)), ACT.Exp,
+                    bias=bias[t][:], scale=rate[:, t : t + 1],
+                )
+
+        def fetch_y():
+            for t in range(4):
+                if t not in Y_ON_VECTOR:
+                    nc.scalar.activation(y_sb[t][:, 0:S], y_bank[t][:], ACT.Copy, scale=2.0)
+                nc.scalar.activation(y_got[:, t, :], y_sb[t][:].indirect(lists["n2"][:]), ACT.Copy)
+
+        def make_gap(ts):
+            for t in ts:
+                nc.vector.scalar_tensor_tensor(
+                    gap[:, t, :], y_bank[t][:], 2.0, y_got[:, t, :], ALU.mult, ALU.subtract
+                )
 
         z_w, z_s = [], []
-        for k, (a, b) in enumerate(Z_PIECES):
+
+        def make_z(k):
+            a, b = Z_PIECES[k]
             n = b - a
-            if k == 0:
-                y_got = sb("y_got0", [P, 4, n], F32)
-            else:
-                y_got = keep.tile([P, 4, n], F32, name="y_got%d" % k, tag="late", align_bytes=64)
-            gap = sb("gap%d" % k, [P, 4, n], F32)
-            ea = sb("ea%d" % k, [P, 4, n], F32)
-            pull = sb("pull%d" % k, [P, 4, n], F32, "pull")
-            z = sb("z%d" % k, [P, 4 * n], BF16, "z")
+            pull = sb("pull%d" % k, [P, 4, n], F32, "pull" if k == len(Z_PIECES) - 1 else None)
+            z = sb("z%d" % k, [P, 4 * n], BF16, None)
             z_w.append(sb("z_w%d" % k, [P, n], U32))
             z_s.append(sb("z_s%d" % k, [P, n], U8))
             for t in range(4):
-                if k == 0:
-                    nc.scalar.copy(y_sb[t][:], y_bank[t][:])
-                nc.scalar.activation(y_got[:, t, :], y_sb[t][:].indirect(offsets(lists["n2"], a, b)), ACT.Copy)
-                nc.vector.tensor_tensor(gap[:, t, :], y_bank[t][:, a:b], y_got[:, t, :], ALU.subtract)
-            for t in range(4):
-                nc.scalar.activation(
-                    ea[:, t, :], d_sb[t][:].indirect(offsets(lists["n1"], a, b)), ACT.Exp,
-                    bias=bias[t][:], scale=vec["tau"][:, t : t + 1],
-                )
                 nc.vector.scalar_tensor_tensor(
-                    pull[:, t, :], gap[:, t, :], gn_twice[:, t : t + 1], ea[:, t, :], ALU.mult, ALU.mult
+                    pull[:, t, :], gap[:, t, a:b], gain[:, t : t + 1], ea[:, t, a:b], ALU.mult, ALU.mult
                 )
             nc.vector.tensor_tensor(woven(z[:]), by_fours(pull[:]), by_fours(d_half[:, :, a:b]), ALU.add)
             nc.vector.quantize_mx(out=z_w[k][:].bitcast(FP8X4), scales=z_s[k][:], in_=z[:])
 
-        h_sb = [sb("h_sb%d" % t, [P, S], F32) for t in range(4)]
-        top2 = [[sb("top2_%d_%d" % (k, t), [P, 1], F32) for t in range(4)] for k in range(len(Z_PIECES))]
-        bias23 = [sb("bias23_%d" % t, [P, 2], F32) for t in range(4)]
-        h_bank = []
-        for k, (a, b) in enumerate(Z_PIECES):
-            h_bank.append([psum.tile([P, S], F32, name="h_bank%d_%d" % (k, t), tag="%s%d" % ("ba"[k], t)) for t in range(4)])
-            for t in range(4):
-                product(h_bank[k][t][:, 0 : b - a], 2, t, z_w[k][:], z_s[k][:])
+        fetch_y()
+        make_gap((0, 1, 2))
         for t in range(4):
-            for k, (a, b) in enumerate(Z_PIECES):
-                before = top2[k - 1][t][:] if k else None
+            nc.vector.tensor_scalar(d_half[:, t, :], d_sb[t][:], gain[:, t : t + 1], -0.5, ALU.mult, ALU.mult)
+        fetch_ea(*Z_PIECES[0])
+        deal_bytes(3)
+        neg_rate23 = sb("neg_rate23", [P, 2, 4], F32)
+        nc.gpsimd.tensor_scalar(neg_rate23[:], rate23[:, :, 0:4], -1.0, 0.0, ALU.mult, ALU.add)
+        make_gap((3,))
+        make_z(0)
+        fetch_ea(*Z_PIECES[1])
+        make_z(1)
+
+        h_sb = [sb("h_sb%d" % t, [P, S], F32, ("pull", "d_half", None, None)[t]) for t in range(4)]
+        top_first = [sb("top_first%d" % t, [P, 1], F32) for t in range(4)]
+        top2 = [sb("top2_%d" % t, [P, 1], F32) for t in range(4)]
+        bias23 = [sb("bias23_%d" % t, [P, 2], F32) for t in range(4)]
+        h_low = [psum.tile([P, S], F32, name="h_low%d" % t, tag="b%d" % t) for t in range(4)]
+        h_high = [psum.tile([P, S], F32, name="h_high%d" % t, tag="a%d" % t) if t in SPLIT_H else h_low[t] for t in range(4)]
+        for k, (a, b) in enumerate(Z_PIECES):
+            for t in range(4):
+                product((h_high if k else h_low)[t][:, a:b], 3, t, z_w[k][:], z_s[k][:])
+        for t in range(4):
+            if t in SPLIT_H:
                 nc.vector.tensor_scalar(
-                    h_sb[t][:, a:b], h_bank[k][t][:, 0 : b - a], 1.0, before, ALU.mult, ALU.max,
-                    accum_out=top2[k][t][:],
+                    h_sb[t][:, 0:256], h_low[t][:, 0:256], 1.0, None, ALU.mult, ALU.max, accum_out=top_first[t][:]
                 )
-            nc.vector.tensor_scalar(bias23[t][:], neg_tau23[:, t, :], top2[-1][t][:], None, ALU.mult)
+                nc.vector.tensor_scalar(
+                    h_sb[t][:, 256:S], h_high[t][:, 256:S], 1.0, top_first[t][:], ALU.mult, ALU.max, accum_out=top2[t][:]
+                )
+            else:
+                nc.vector.tensor_scalar(h_sb[t][:], h_low[t][:], 1.0, None, ALU.mult, ALU.max, accum_out=top2[t][:])
+            if t in BIAS_ON_SCALAR:
+                nc.scalar.activation(bias23[t][:], neg_rate23[:, :, t], ACT.Copy, scale=top2[t][:])
+            else:
+                nc.vector.tensor_scalar(bias23[t][:], neg_rate23[:, :, t], top2[t][:], None, ALU.mult)
 
         out_w = sb("out_w", [P, S], U32)
         out_s = sb("out_s", [P, S], U8)
@@ -214,10 +248,10 @@ def tile_picked_twlpxbetw_none_po_kernel(
             res = sb("res%d" % k, [P, 4, n], F32)
             rounded = sb("rounded%d" % k, [P, 4 * n], BF16, "rounded")
             for t in range(4):
-                for got, lst, rate, col in ((ea2, "n3", "tau2", 0), (ea3, "n4", "tau3", 1)):
+                for got, lst, col in ((ea2, "n3", 0), (ea3, "n4", 1)):
                     nc.scalar.activation(
                         got[:, t, :], h_sb[t][:].indirect(offsets(lists[lst], a, b)), ACT.Exp,
-                        bias=bias23[t][:, col : col + 1], scale=vec[rate][:, t : t + 1],
+                        bias=bias23[t][:, col : col + 1], scale=rate23[:, col, t : t + 1],
                     )
                 nc.vector.tensor_tensor(diff[:, t, :], ea2[:, t, :], ea3[:, t, :], ALU.subtract)
             nc.vector.tensor_scalar(woven(rounded[:]), by_fours(diff[:]), 3.0, None, ALU.mult)

@@ -17,11 +17,12 @@ ACT = mybir.ActivationFunctionType
 
 P = 128
 Z_PIECES = ((0, 256), (256, 512))
-OUT_PIECES = ((0, 256), (256, 384), (384, 512))
+OUT_PIECES = ((0, 256), (256, 512))
 Y_ON_VECTOR = (2,)
 SPLIT_H = (0, 1)
 BIAS_ON_SCALAR = (0,)
 SPARE = 16
+WIDE = (0, 1, 2)
 HALF_ON_SCALAR = ()
 
 
@@ -84,28 +85,30 @@ def tile_picked_twlpxbetw_none_po_kernel(
         y_sb = [sb("y_sb%d" % t, [P, S + SPARE], F32) for t in range(4)]
         for t in range(4):
             nc.vector.memset(y_sb[t][:, S:], 0.0)
+        h_sb = [sb("h_sb%d" % t, [P, 2 * S if t in WIDE else S], F32) for t in range(4)]
         nc.scalar.dma_start(out=rate[:], in_=by_rows(tau))
         load_scale_rows(nc.scalar, xs, x_scales, (0, 2))
         nc.scalar.dma_start(out=xw[:].bitcast(I32), in_=words_of(x_words))
-        nc.scalar.dma_start(out=raw_w[1][:].bitcast(I32), in_=words_of(w1_words))
-        nc.scalar.dma_start(out=raw_w[2][:].bitcast(I32), in_=words_of(w2_words))
+        load_scale_rows(nc.scalar, raw_s[2], w2_scales, (0,))
+        nc.scalar.dma_start(out=raw_w[3][:].bitcast(I32), in_=words_of(w3_words))
         nc.scalar.activation(neg_rate[:], rate[:], ACT.Copy, scale=-1.0)
         nc.sync.dma_start(lists["offs"][:], offs)
         nc.sync.dma_start(lists["two"][:], two)
         load_scale_rows(nc.sync, xs, x_scales, (1, 3))
         load_scale_rows(nc.sync, raw_s[1], w1_scales, (0, 1, 2))
-        load_scale_rows(nc.sync, raw_s[2], w2_scales, (0, 1, 2))
+        nc.sync.dma_start(out=raw_w[1][:].bitcast(I32), in_=words_of(w1_words))
+        nc.sync.dma_start(out=raw_w[2][:].bitcast(I32), in_=words_of(w2_words))
+        load_scale_rows(nc.sync, raw_s[2], w2_scales, (1,))
         nc.sync.dma_start(lists["n2"][:], n2)
         nc.sync.dma_start(lists["n1"][:], n1)
+        nc.sync.dma_start(out=gain[:], in_=by_rows(gn))
         load_scale_rows(nc.sync, raw_s[3], w3_scales, range(4))
         nc.sync.dma_start(lists["n3"][:], n3)
         nc.sync.dma_start(lists["n4"][:], n4)
         for j, column in enumerate((tau2, tau3)):
             nc.sync.dma_start(out=rate23[:, j, 0:4], in_=by_rows(column))
-        nc.gpsimd.dma_start(out=gain[:], in_=by_rows(gn))
         load_scale_rows(nc.gpsimd, raw_s[1], w1_scales, (3,))
-        load_scale_rows(nc.gpsimd, raw_s[2], w2_scales, (3,))
-        nc.gpsimd.dma_start(out=raw_w[3][:].bitcast(I32), in_=words_of(w3_words))
+        load_scale_rows(nc.gpsimd, raw_s[2], w2_scales, (2, 3))
 
         def deal_words(engine_copy, i):
             engine_copy(
@@ -161,14 +164,15 @@ def tile_picked_twlpxbetw_none_po_kernel(
             nc.vector.tensor_scalar(half_gain[:], gain[:], -0.5, None, ALU.mult)
 
         HALVES = ((0, 256), (256, 512))
-        ea = sb("ea", [P, 4, S], F32)
+        ea = [sb("ea%d" % k, [P, 4, b - a], F32, "top3" if k == 1 else None) for k, (a, b) in enumerate(Z_PIECES)]
         y_got = sb("y_got", [P, 4, S], F32)
-        gap = sb("gap", [P, 4, S], F32)
+        gap = [h_sb[t][:, S:] if t in WIDE else sb("gap%d" % t, [P, S], F32)[:] for t in range(4)]
 
-        def fetch_ea(a, b):
+        def fetch_ea(k):
+            a, b = Z_PIECES[k]
             for t in range(4):
                 nc.scalar.activation(
-                    ea[:, t, a:b], d_sb[t][:].indirect(offsets(lists["n1"], a, b)), ACT.Exp,
+                    ea[k][:, t, :], d_sb[t][:].indirect(offsets(lists["n1"], a, b)), ACT.Exp,
                     bias=bias[t][:], scale=rate[:, t : t + 1],
                 )
 
@@ -181,7 +185,7 @@ def tile_picked_twlpxbetw_none_po_kernel(
         def make_gap(ts):
             for t in ts:
                 nc.vector.scalar_tensor_tensor(
-                    gap[:, t, :], y_bank[t][:], 2.0, y_got[:, t, :], ALU.mult, ALU.subtract
+                    gap[t], y_bank[t][:], 2.0, y_got[:, t, :], ALU.mult, ALU.subtract
                 )
 
         z_w, z_s = [], []
@@ -195,7 +199,7 @@ def tile_picked_twlpxbetw_none_po_kernel(
             z_s.append(sb("z_s%d" % k, [P, n], U8))
             for t in range(4):
                 nc.vector.scalar_tensor_tensor(
-                    pull[:, t, :], gap[:, t, a:b], gain[:, t : t + 1], ea[:, t, a:b], ALU.mult, ALU.mult
+                    pull[:, t, :], gap[t][:, a:b], gain[:, t : t + 1], ea[k][:, t, :], ALU.mult, ALU.mult
                 )
             nc.vector.tensor_tensor(woven(z[:]), by_fours(pull[:]), by_fours(d_half[:, :, a:b]), ALU.add)
             nc.vector.quantize_mx(out=z_w[k][:].bitcast(FP8X4), scales=z_s[k][:], in_=z[:])
@@ -204,17 +208,16 @@ def tile_picked_twlpxbetw_none_po_kernel(
         make_gap((0, 1, 2))
         for t in range(4):
             nc.vector.tensor_scalar(d_half[:, t, :], d_sb[t][:], gain[:, t : t + 1], -0.5, ALU.mult, ALU.mult)
-        fetch_ea(*Z_PIECES[0])
+        fetch_ea(0)
         deal_bytes(3)
         neg_rate23 = sb("neg_rate23", [P, 2, 4], F32)
         nc.gpsimd.tensor_scalar(neg_rate23[:], rate23[:, :, 0:4], -1.0, 0.0, ALU.mult, ALU.add)
         make_gap((3,))
         make_z(0)
-        fetch_ea(*Z_PIECES[1])
+        fetch_ea(1)
         make_z(1)
 
-        h_sb = [sb("h_sb%d" % t, [P, S], F32, ("pull", "d_half", None, None)[t]) for t in range(4)]
-        top_first = [sb("top_first%d" % t, [P, 1], F32) for t in range(4)]
+        top_first = [sb("top_first%d" % t, [P, 1], F32, ("pull", "d_half", None, None)[t]) for t in range(4)]
         top2 = [sb("top2_%d" % t, [P, 1], F32) for t in range(4)]
         bias23 = [sb("bias23_%d" % t, [P, 2], F32) for t in range(4)]
         h_low = [psum.tile([P, S], F32, name="h_low%d" % t, tag="b%d" % t) for t in range(4)]
@@ -231,7 +234,7 @@ def tile_picked_twlpxbetw_none_po_kernel(
                     h_sb[t][:, 256:S], h_high[t][:, 256:S], 1.0, top_first[t][:], ALU.mult, ALU.max, accum_out=top2[t][:]
                 )
             else:
-                nc.vector.tensor_scalar(h_sb[t][:], h_low[t][:], 1.0, None, ALU.mult, ALU.max, accum_out=top2[t][:])
+                nc.vector.tensor_scalar(h_sb[t][:, 0:S], h_low[t][:], 1.0, None, ALU.mult, ALU.max, accum_out=top2[t][:])
             if t in BIAS_ON_SCALAR:
                 nc.scalar.activation(bias23[t][:], neg_rate23[:, :, t], ACT.Copy, scale=top2[t][:])
             else:
@@ -240,28 +243,39 @@ def tile_picked_twlpxbetw_none_po_kernel(
         out_w = sb("out_w", [P, S], U32)
         out_s = sb("out_s", [P, S], U8)
         rows = out_0.rearrange("(p t) j -> p t j", t=4)
-        for k, (a, b) in enumerate(OUT_PIECES):
-            n = b - a
-            ea2 = sb("ea2_%d" % k, [P, 4, n], F32)
-            ea3 = sb("ea3_%d" % k, [P, 4, n], F32)
-            diff = sb("diff%d" % k, [P, 4, n], F32)
-            res = sb("res%d" % k, [P, 4, n], F32)
-            rounded = sb("rounded%d" % k, [P, 4 * n], BF16, "rounded")
-            for t in range(4):
-                for got, lst, col in ((ea2, "n3", 0), (ea3, "n4", 1)):
-                    nc.scalar.activation(
-                        got[:, t, :], h_sb[t][:].indirect(offsets(lists[lst], a, b)), ACT.Exp,
-                        bias=bias23[t][:, col : col + 1], scale=rate23[:, col, t : t + 1],
-                    )
-                nc.vector.tensor_tensor(diff[:, t, :], ea2[:, t, :], ea3[:, t, :], ALU.subtract)
-            nc.vector.tensor_scalar(woven(rounded[:]), by_fours(diff[:]), 3.0, None, ALU.mult)
-            if k == len(OUT_PIECES) - 1:
-                nc.scalar.activation(res[:], diff[:], ACT.Copy, scale=3.0)
+        ea2 = sb("ea2", [P, 4, S], F32)
+        ea3 = sb("ea3", [P, 4, S], F32)
+        diff = sb("diff", [P, 4, S], F32)
+        res = sb("res", [P, 4, S], F32)
+
+        def finish(t, a, b, last):
+            for got, lst, col in ((ea2, "n3", 0), (ea3, "n4", 1)):
+                nc.scalar.activation(
+                    got[:, t, a:b], h_sb[t][:].indirect(offsets(lists[lst], a, b)), ACT.Exp,
+                    bias=bias23[t][:, col : col + 1], scale=rate23[:, col, t : t + 1],
+                )
+            nc.vector.tensor_tensor(diff[:, t, a:b], ea2[:, t, a:b], ea3[:, t, a:b], ALU.subtract)
+
+        def store(t, a, b, last):
+            if last:
+                nc.scalar.activation(res[:, t, a:b], diff[:, t, a:b], ACT.Copy, scale=3.0)
             else:
-                nc.vector.tensor_scalar(res[:], diff[:], 3.0, None, ALU.mult)
+                nc.vector.tensor_scalar(res[:, t, a:b], diff[:, t, a:b], 3.0, None, ALU.mult)
+            nc.sync.dma_start(out=rows[:, t, a:b], in_=res[:, t, a:b])
+
+        for t in WIDE:
+            finish(t, 0, S, False)
+            store(t, 0, S, False)
+        narrow = slice(len(WIDE), 4)
+        for k, (a, b) in enumerate(OUT_PIECES):
+            last = k == len(OUT_PIECES) - 1
+            rounded = sb("rounded%d" % k, [P, 4 * (b - a)], BF16)
+            for t in range(len(WIDE), 4):
+                finish(t, a, b, last)
+            nc.vector.tensor_scalar(woven(rounded[:]), by_fours(diff[:, :, a:b]), 3.0, None, ALU.mult)
             nc.vector.quantize_mx(out=out_w[:, a:b].bitcast(FP8X4), scales=out_s[:, a:b], in_=rounded[:])
-            nc.sync.dma_start(out=rows[:, :, a:b], in_=res[:])
             nc.sync.dma_start(out=words_of(out_1)[:, a:b], in_=out_w[:, a:b].bitcast(I32))
+            store(narrow, a, b, last)
         for q in range(4):
             queue = nc.scalar if q % 2 else nc.sync
             queue.dma_start(

@@ -2,8 +2,9 @@ from contextlib import ExitStack
 
 import concourse.mybir as mybir
 
-K, T, S, N, H = 512, 2048, 512, 512, 512
-FLOPS = 3 * 2 * 512 * 512 * 512
+T, S = 2048, 512
+WIDTH = 512
+FLOPS = 3 * 2 * 512 * WIDTH * S
 
 F32 = mybir.dt.float32
 BF16 = mybir.dt.bfloat16
@@ -16,14 +17,13 @@ ALU = mybir.AluOpType
 ACT = mybir.ActivationFunctionType
 
 P = 128
-Z_PIECES = ((0, 256), (256, 512))
-OUT_PIECES = ((0, 256), (256, 512))
-Y_ON_VECTOR = (2,)
-SPLIT_H = (0, 1)
-BIAS_ON_SCALAR = (0,)
+PACK = 4
+HALF = S // 2
+HALVES = ((0, HALF), (HALF, S))
+LAST = PACK - 1
+Y_ON_VECTOR = (2, 3)
+H_IN_HALVES = (0, 1)
 SPARE = 16
-WIDE = (0, 1, 2)
-HALF_ON_SCALAR = ()
 
 
 def words_of(dram):
@@ -31,7 +31,7 @@ def words_of(dram):
 
 
 def by_rows(column):
-    return column.rearrange("(p t) o -> p (t o)", t=4)
+    return column.rearrange("(p t) o -> p (t o)", t=PACK)
 
 
 def load_scale_rows(queue, tile, dram, quadrants):
@@ -47,7 +47,7 @@ def offsets(lst, a, b):
 
 
 def woven(ap):
-    return ap.rearrange("p (c i t) -> p c t i", i=4, t=4)
+    return ap.rearrange("p (c i t) -> p c t i", i=4, t=PACK)
 
 
 def by_fours(ap):
@@ -63,42 +63,42 @@ def tile_picked_twlpxbetw_none_po_kernel(
         keep = ctx.enter_context(tc.tile_pool(name="keep", bufs=1))
         psum = ctx.enter_context(tc.psum_pool(name="psum", bufs=1))
 
-        def sb(name, shape, dt, tag=None):
-            return keep.tile(shape, dt, name=name, tag=tag or name, align_bytes=64)
+        def sb(name, shape, dtype, tag=None):
+            return keep.tile(shape, dtype, name=name, tag=tag or name, align_bytes=64)
 
         lists = {nm: keep.tile([P, S // 16], U16, name="list_" + nm) for nm in ("offs", "two", "n1", "n2", "n3", "n4")}
         xw = sb("xw", [P, T], U32)
         xs = sb("xs", [P, T], U8)
-        raw_w = {i: sb("raw_w%d" % i, [P, 512], U32) for i in (1, 2, 3)}
-        dealt_w = {i: sb("dealt_w%d" % i, [P, 512], U32) for i in (1, 2, 3)}
-        raw_s = {i: sb("raw_s%d" % i, [P, 512], U8) for i in (1, 2, 3)}
-        dealt_s = {i: sb("dealt_s%d" % i, [P, 512], U8) for i in (1, 2, 3)}
-        rate = sb("rate", [P, 4], F32)
-        gain = sb("gain", [P, 4], F32)
-        neg_rate = sb("neg_rate", [P, 4], F32)
+        raw_w = {i: sb("raw_w%d" % i, [P, WIDTH], U32) for i in (1, 2, 3)}
+        dealt_w = {i: sb("dealt_w%d" % i, [P, WIDTH], U32) for i in (1, 2, 3)}
+        raw_s = {i: sb("raw_s%d" % i, [P, WIDTH], U8) for i in (1, 2, 3)}
+        dealt_s = {i: sb("dealt_s%d" % i, [P, WIDTH], U8) for i in (1, 2, 3)}
+        rate = sb("rate", [P, PACK], F32)
+        gain = sb("gain", [P, PACK], F32)
+        neg_rate = sb("neg_rate", [P, PACK], F32)
         rate23 = sb("rate23", [P, 2, 8], F32)
+        y_sb = [sb("y_sb%d" % t, [P, S + SPARE], F32) for t in range(PACK)]
+        h_sb = [sb("h_sb%d" % t, [P, S if t == LAST else 2 * S], F32) for t in range(PACK)]
 
         nc.vector.memset(xs[:, 0 : T // 2].bitcast(I32), 0)
         nc.gpsimd.memset(xs[:, T // 2 : T].bitcast(I32), 0)
-        for i in (1, 2, 3):
+        for i in (2, 1, 3):
             nc.vector.memset(raw_s[i][:].bitcast(I32), 0)
-        y_sb = [sb("y_sb%d" % t, [P, S + SPARE], F32) for t in range(4)]
-        for t in range(4):
+        for t in range(PACK):
             nc.vector.memset(y_sb[t][:, S:], 0.0)
-        h_sb = [sb("h_sb%d" % t, [P, 2 * S if t in WIDE else S], F32) for t in range(4)]
+
         nc.scalar.dma_start(out=rate[:], in_=by_rows(tau))
         load_scale_rows(nc.scalar, xs, x_scales, (0, 2))
         nc.scalar.dma_start(out=xw[:].bitcast(I32), in_=words_of(x_words))
-        load_scale_rows(nc.scalar, raw_s[2], w2_scales, (0,))
-        nc.scalar.dma_start(out=raw_w[3][:].bitcast(I32), in_=words_of(w3_words))
+        nc.scalar.dma_start(out=raw_w[1][:].bitcast(I32), in_=words_of(w1_words))
+        nc.scalar.dma_start(out=raw_w[2][:].bitcast(I32), in_=words_of(w2_words))
         nc.scalar.activation(neg_rate[:], rate[:], ACT.Copy, scale=-1.0)
         nc.sync.dma_start(lists["offs"][:], offs)
         nc.sync.dma_start(lists["two"][:], two)
         load_scale_rows(nc.sync, xs, x_scales, (1, 3))
-        load_scale_rows(nc.sync, raw_s[1], w1_scales, (0, 1, 2))
-        nc.sync.dma_start(out=raw_w[1][:].bitcast(I32), in_=words_of(w1_words))
-        nc.sync.dma_start(out=raw_w[2][:].bitcast(I32), in_=words_of(w2_words))
-        load_scale_rows(nc.sync, raw_s[2], w2_scales, (1,))
+        load_scale_rows(nc.sync, raw_s[1], w1_scales, range(4))
+        nc.sync.dma_start(out=raw_w[3][:].bitcast(I32), in_=words_of(w3_words))
+        load_scale_rows(nc.sync, raw_s[2], w2_scales, (0,))
         nc.sync.dma_start(lists["n2"][:], n2)
         nc.sync.dma_start(lists["n1"][:], n1)
         nc.sync.dma_start(out=gain[:], in_=by_rows(gn))
@@ -106,178 +106,160 @@ def tile_picked_twlpxbetw_none_po_kernel(
         nc.sync.dma_start(lists["n3"][:], n3)
         nc.sync.dma_start(lists["n4"][:], n4)
         for j, column in enumerate((tau2, tau3)):
-            nc.sync.dma_start(out=rate23[:, j, 0:4], in_=by_rows(column))
-        load_scale_rows(nc.gpsimd, raw_s[1], w1_scales, (3,))
-        load_scale_rows(nc.gpsimd, raw_s[2], w2_scales, (2, 3))
+            nc.sync.dma_start(out=rate23[:, j, 0:PACK], in_=by_rows(column))
+        load_scale_rows(nc.gpsimd, raw_s[2], w2_scales, (1, 2, 3))
 
-        def deal_words(engine_copy, i):
-            engine_copy(
-                out=dealt_w[i][:].rearrange("p (t m) -> p m t", t=4),
-                in_=raw_w[i][:].rearrange("p (m t) -> p m t", t=4),
-            )
-
-        def deal_bytes(i):
-            (nc.gpsimd if i == 3 else nc.vector).tensor_copy(
-                out=dealt_s[i][:].rearrange("p (t m) -> p t m", t=4),
-                in_=raw_s[i][:].rearrange("p (m t) -> p t m", t=4),
+        def deal_bytes(engine, i):
+            engine.tensor_copy(
+                out=dealt_s[i][:].rearrange("p (t m) -> p t m", t=PACK),
+                in_=raw_s[i][:].rearrange("p (m t) -> p t m", t=PACK),
             )
 
         def product(bank, i, t, words, scales):
-            cols = slice(128 * t, 128 * (t + 1))
+            cols = slice(P * t, P * (t + 1))
             nc.tensor.matmul_mx(
                 out=bank, lhsT=dealt_w[i][:, cols].bitcast(FP8X4), lhsT_scale=dealt_s[i][:, cols],
                 rhs=words.bitcast(FP8X4), rhs_scale=scales, start=True, stop=True,
             )
 
-        picked_w = {nm: sb("picked_w_" + nm, [P, S], U32) for nm in ("two", "offs")}
-        picked_s = {nm: sb("picked_s_" + nm, [P, S], U8) for nm in ("two", "offs")}
+        picked_s = {nm: sb("picked_s_" + nm, [P, S], U8) for nm in ("offs", "two")}
         for nm in ("offs", "two"):
             nc.vector.tensor_copy(picked_s[nm][:], xs[:].indirect(lists[nm][:]))
-        deal_bytes(1)
         for i in (1, 2, 3):
-            deal_words(nc.scalar.copy, i)
-        for nm in ("offs", "two"):
-            nc.vector.tensor_copy(picked_w[nm][:], xw[:].indirect(lists[nm][:]))
-        deal_bytes(2)
-        d_bank = [psum.tile([P, S], F32, name="d_bank%d" % t, tag="b%d" % t) for t in range(4)]
-        y_bank = [psum.tile([P, S], F32, name="y_bank%d" % t, tag="a%d" % t) for t in range(4)]
-        for step in "y0 y1 d0 y2 d1 y3 d2 d3".split():
-            t = int(step[1])
-            if step[0] == "y":
-                product(y_bank[t][:], 1, t, picked_w["offs"][:], picked_s["offs"][:])
-            else:
-                product(d_bank[t][:], 2, t, picked_w["two"][:], picked_s["two"][:])
+            nc.scalar.copy(
+                out=dealt_w[i][:].rearrange("p (t m) -> p m t", t=PACK),
+                in_=raw_w[i][:].rearrange("p (m t) -> p m t", t=PACK),
+            )
+        offs_words = sb("offs_words", [P, S], U32)
+        nc.vector.tensor_copy(offs_words[:], xw[:].indirect(lists["offs"][:]))
+        deal_bytes(nc.vector, 1)
+        two_words = sb("two_words", [P, S], U32, tag="raw_s1")
+        nc.vector.tensor_copy(two_words[:], xw[:].indirect(lists["two"][:]))
+        deal_bytes(nc.vector, 2)
 
+        d_bank = [psum.tile([P, S], F32, name="d_bank%d" % t, tag="d%d" % t) for t in range(PACK)]
+        y_bank = [psum.tile([P, S], F32, name="y_bank%d" % t, tag="y%d" % t) for t in range(PACK)]
+        for t in range(PACK):
+            product(y_bank[t][:], 1, t, offs_words[:], picked_s["offs"][:])
+        for t in range(PACK):
+            product(d_bank[t][:], 2, t, two_words[:], picked_s["two"][:])
 
-        d_sb = [sb("d_sb%d" % t, [P, S], F32) for t in range(4)]
-        top = [sb("top%d" % t, [P, 1], F32) for t in range(4)]
-        bias = [sb("bias%d" % t, [P, 1], F32) for t in range(4)]
-        d_half = sb("d_half", [P, 4, S], F32)
-        half_gain = sb("half_gain", [P, 4], F32)
-
+        d_sb = [sb("d_sb%d" % t, [P, S], F32) for t in range(PACK)]
+        top = [sb("top%d" % t, [P, 1], F32) for t in range(PACK)]
+        bias = [sb("bias%d" % t, [P, 1], F32) for t in range(PACK)]
         for t in Y_ON_VECTOR:
             nc.vector.tensor_scalar(y_sb[t][:, 0:S], y_bank[t][:], 2.0, None, ALU.mult)
-        for t in range(4):
+        for t in range(PACK):
             nc.vector.tensor_scalar(d_sb[t][:], d_bank[t][:], 1.0, None, ALU.mult, ALU.max, accum_out=top[t][:])
             nc.vector.tensor_scalar(bias[t][:], top[t][:], neg_rate[:, t : t + 1], None, ALU.mult)
-        if HALF_ON_SCALAR:
-            nc.vector.tensor_scalar(half_gain[:], gain[:], -0.5, None, ALU.mult)
 
-        HALVES = ((0, 256), (256, 512))
-        ea = [sb("ea%d" % k, [P, 4, b - a], F32, "top3" if k == 1 else None) for k, (a, b) in enumerate(Z_PIECES)]
-        y_got = sb("y_got", [P, 4, S], F32)
-        gap = [h_sb[t][:, S:] if t in WIDE else sb("gap%d" % t, [P, S], F32)[:] for t in range(4)]
+        y_got = sb("y_got", [P, PACK, S], F32)
+        for t in range(PACK):
+            if t not in Y_ON_VECTOR:
+                nc.scalar.activation(y_sb[t][:, 0:S], y_bank[t][:], ACT.Copy, scale=2.0)
+            nc.scalar.activation(y_got[:, t, :], y_sb[t][:].indirect(lists["n2"][:]), ACT.Copy)
 
-        def fetch_ea(k):
-            a, b = Z_PIECES[k]
-            for t in range(4):
+        d_half = sb("d_half", [P, PACK, S], F32)
+        for t in range(PACK):
+            nc.gpsimd.tensor_scalar(d_half[:, t, :], d_sb[t][:], gain[:, t : t + 1], -0.5, ALU.mult, ALU.mult)
+
+        def fetch_ea(k, tag):
+            a, b = HALVES[k]
+            ea = sb("ea%d" % k, [P, PACK, HALF], F32, tag)
+            for t in range(PACK):
                 nc.scalar.activation(
-                    ea[k][:, t, :], d_sb[t][:].indirect(offsets(lists["n1"], a, b)), ACT.Exp,
+                    ea[:, t, :], d_sb[t][:].indirect(offsets(lists["n1"], a, b)), ACT.Exp,
                     bias=bias[t][:], scale=rate[:, t : t + 1],
                 )
+            return ea
 
-        def fetch_y():
-            for t in range(4):
-                if t not in Y_ON_VECTOR:
-                    nc.scalar.activation(y_sb[t][:, 0:S], y_bank[t][:], ACT.Copy, scale=2.0)
-                nc.scalar.activation(y_got[:, t, :], y_sb[t][:].indirect(lists["n2"][:]), ACT.Copy)
-
-        def make_gap(ts):
-            for t in ts:
+        def make_z(k, ea):
+            a, b = HALVES[k]
+            pull = sb("pull%d" % k, [P, PACK, HALF], F32, tag="pull")
+            z = sb("z%d" % k, [P, PACK * HALF], BF16)
+            words = sb("z_words%d" % k, [P, HALF], U32)
+            scales = sb("z_scales%d" % k, [P, HALF], U8)
+            for t in range(PACK):
                 nc.vector.scalar_tensor_tensor(
-                    gap[t], y_bank[t][:], 2.0, y_got[:, t, :], ALU.mult, ALU.subtract
-                )
-
-        z_w, z_s = [], []
-
-        def make_z(k):
-            a, b = Z_PIECES[k]
-            n = b - a
-            pull = sb("pull%d" % k, [P, 4, n], F32, "pull" if k == len(Z_PIECES) - 1 else None)
-            z = sb("z%d" % k, [P, 4 * n], BF16, None)
-            z_w.append(sb("z_w%d" % k, [P, n], U32))
-            z_s.append(sb("z_s%d" % k, [P, n], U8))
-            for t in range(4):
-                nc.vector.scalar_tensor_tensor(
-                    pull[:, t, :], gap[t][:, a:b], gain[:, t : t + 1], ea[k][:, t, :], ALU.mult, ALU.mult
+                    pull[:, t, :], gap[t][:, a:b], gain[:, t : t + 1], ea[:, t, :], ALU.mult, ALU.mult
                 )
             nc.vector.tensor_tensor(woven(z[:]), by_fours(pull[:]), by_fours(d_half[:, :, a:b]), ALU.add)
-            nc.vector.quantize_mx(out=z_w[k][:].bitcast(FP8X4), scales=z_s[k][:], in_=z[:])
+            nc.vector.quantize_mx(out=words[:].bitcast(FP8X4), scales=scales[:], in_=z[:])
+            return words, scales
 
-        fetch_y()
-        make_gap((0, 1, 2))
-        for t in range(4):
-            nc.vector.tensor_scalar(d_half[:, t, :], d_sb[t][:], gain[:, t : t + 1], -0.5, ALU.mult, ALU.mult)
-        fetch_ea(0)
-        deal_bytes(3)
-        neg_rate23 = sb("neg_rate23", [P, 2, 4], F32)
-        nc.gpsimd.tensor_scalar(neg_rate23[:], rate23[:, :, 0:4], -1.0, 0.0, ALU.mult, ALU.add)
-        make_gap((3,))
-        make_z(0)
-        fetch_ea(1)
-        make_z(1)
+        ea_low = fetch_ea(0, None)
+        deal_bytes(nc.gpsimd, 3)
+        neg_rate23 = sb("neg_rate23", [P, 2, PACK], F32)
+        nc.gpsimd.tensor_scalar(neg_rate23[:], rate23[:, :, 0:PACK], -1.0, 0.0, ALU.mult, ALU.add)
+        gap = [sb("gap_last", [P, S], F32)[:] if t == LAST else h_sb[t][:, S:] for t in range(PACK)]
+        for t in range(PACK):
+            nc.vector.scalar_tensor_tensor(gap[t], y_bank[t][:], 2.0, y_got[:, t, :], ALU.mult, ALU.subtract)
+        z_low = make_z(0, ea_low)
+        ea_high = fetch_ea(1, "top%d" % LAST)
+        z_high = make_z(1, ea_high)
 
-        top_first = [sb("top_first%d" % t, [P, 1], F32, ("pull", "d_half", None, None)[t]) for t in range(4)]
-        top2 = [sb("top2_%d" % t, [P, 1], F32) for t in range(4)]
-        bias23 = [sb("bias23_%d" % t, [P, 2], F32) for t in range(4)]
-        h_low = [psum.tile([P, S], F32, name="h_low%d" % t, tag="b%d" % t) for t in range(4)]
-        h_high = [psum.tile([P, S], F32, name="h_high%d" % t, tag="a%d" % t) if t in SPLIT_H else h_low[t] for t in range(4)]
-        for k, (a, b) in enumerate(Z_PIECES):
-            for t in range(4):
-                product((h_high if k else h_low)[t][:, a:b], 3, t, z_w[k][:], z_s[k][:])
-        for t in range(4):
-            if t in SPLIT_H:
+        h_low = [psum.tile([P, S], F32, name="h_low%d" % t, tag="d%d" % t) for t in range(PACK)]
+        h_high = [
+            psum.tile([P, S], F32, name="h_high%d" % t, tag="y%d" % t) if t in H_IN_HALVES else h_low[t]
+            for t in range(PACK)
+        ]
+        for t in range(PACK):
+            product(h_low[t][:, 0:HALF], 3, t, z_low[0][:], z_low[1][:])
+        for t in range(PACK):
+            product(h_high[t][:, HALF:S], 3, t, z_high[0][:], z_high[1][:])
+
+        top_low = [sb("top_low%d" % t, [P, 1], F32, tag) for t, tag in zip(H_IN_HALVES, ("pull", "d_half"))]
+        top2 = [sb("top2_%d" % t, [P, 1], F32) for t in range(PACK)]
+        bias23 = [sb("bias23_%d" % t, [P, 2], F32) for t in range(PACK)]
+        for t in range(PACK):
+            if t in H_IN_HALVES:
                 nc.vector.tensor_scalar(
-                    h_sb[t][:, 0:256], h_low[t][:, 0:256], 1.0, None, ALU.mult, ALU.max, accum_out=top_first[t][:]
+                    h_sb[t][:, 0:HALF], h_low[t][:, 0:HALF], 1.0, None, ALU.mult, ALU.max, accum_out=top_low[t][:]
                 )
                 nc.vector.tensor_scalar(
-                    h_sb[t][:, 256:S], h_high[t][:, 256:S], 1.0, top_first[t][:], ALU.mult, ALU.max, accum_out=top2[t][:]
+                    h_sb[t][:, HALF:S], h_high[t][:, HALF:S], 1.0, top_low[t][:], ALU.mult, ALU.max,
+                    accum_out=top2[t][:],
                 )
             else:
                 nc.vector.tensor_scalar(h_sb[t][:, 0:S], h_low[t][:], 1.0, None, ALU.mult, ALU.max, accum_out=top2[t][:])
-            if t in BIAS_ON_SCALAR:
+            if t == 0:
                 nc.scalar.activation(bias23[t][:], neg_rate23[:, :, t], ACT.Copy, scale=top2[t][:])
             else:
                 nc.vector.tensor_scalar(bias23[t][:], neg_rate23[:, :, t], top2[t][:], None, ALU.mult)
 
-        out_w = sb("out_w", [P, S], U32)
-        out_s = sb("out_s", [P, S], U8)
-        rows = out_0.rearrange("(p t) j -> p t j", t=4)
-        ea2 = sb("ea2", [P, 4, S], F32)
-        ea3 = sb("ea3", [P, 4, S], F32)
-        diff = sb("diff", [P, 4, S], F32)
-        res = sb("res", [P, 4, S], F32)
+        out_words = sb("out_words", [P, S], U32)
+        out_scales = sb("out_scales", [P, S], U8)
+        ea2 = sb("ea2", [P, PACK, S], F32)
+        ea3 = sb("ea3", [P, PACK, S], F32)
+        diff = sb("diff", [P, PACK, S], F32)
+        res = sb("res", [P, PACK, S], F32)
+        rows = out_0.rearrange("(p t) j -> p t j", t=PACK)
 
-        def finish(t, a, b, last):
-            for got, lst, col in ((ea2, "n3", 0), (ea3, "n4", 1)):
+        def make_diff(t, a, b):
+            for got, lst, j in ((ea2, "n3", 0), (ea3, "n4", 1)):
                 nc.scalar.activation(
                     got[:, t, a:b], h_sb[t][:].indirect(offsets(lists[lst], a, b)), ACT.Exp,
-                    bias=bias23[t][:, col : col + 1], scale=rate23[:, col, t : t + 1],
+                    bias=bias23[t][:, j : j + 1], scale=rate23[:, j, t : t + 1],
                 )
             nc.vector.tensor_tensor(diff[:, t, a:b], ea2[:, t, a:b], ea3[:, t, a:b], ALU.subtract)
 
-        def store(t, a, b, last):
-            if last:
-                nc.scalar.activation(res[:, t, a:b], diff[:, t, a:b], ACT.Copy, scale=3.0)
-            else:
-                nc.vector.tensor_scalar(res[:, t, a:b], diff[:, t, a:b], 3.0, None, ALU.mult)
-            nc.sync.dma_start(out=rows[:, t, a:b], in_=res[:, t, a:b])
-
-        for t in WIDE:
-            finish(t, 0, S, False)
-            store(t, 0, S, False)
-        narrow = slice(len(WIDE), 4)
-        for k, (a, b) in enumerate(OUT_PIECES):
-            last = k == len(OUT_PIECES) - 1
-            rounded = sb("rounded%d" % k, [P, 4 * (b - a)], BF16)
-            for t in range(len(WIDE), 4):
-                finish(t, a, b, last)
+        for t in range(LAST):
+            make_diff(t, 0, S)
+            nc.vector.tensor_scalar(res[:, t, :], diff[:, t, :], 3.0, None, ALU.mult)
+            nc.sync.dma_start(out=rows[:, t, :], in_=res[:, t, :])
+        for k, (a, b) in enumerate(HALVES):
+            make_diff(LAST, a, b)
+            rounded = sb("rounded%d" % k, [P, PACK * HALF], BF16)
             nc.vector.tensor_scalar(woven(rounded[:]), by_fours(diff[:, :, a:b]), 3.0, None, ALU.mult)
-            nc.vector.quantize_mx(out=out_w[:, a:b].bitcast(FP8X4), scales=out_s[:, a:b], in_=rounded[:])
-            nc.sync.dma_start(out=words_of(out_1)[:, a:b], in_=out_w[:, a:b].bitcast(I32))
-            store(narrow, a, b, last)
+            nc.vector.quantize_mx(out=out_words[:, a:b].bitcast(FP8X4), scales=out_scales[:, a:b], in_=rounded[:])
+            nc.sync.dma_start(out=words_of(out_1)[:, a:b], in_=out_words[:, a:b].bitcast(I32))
+            if b == S:
+                nc.scalar.activation(res[:, LAST, a:b], diff[:, LAST, a:b], ACT.Copy, scale=3.0)
+            else:
+                nc.vector.tensor_scalar(res[:, LAST, a:b], diff[:, LAST, a:b], 3.0, None, ALU.mult)
+            nc.sync.dma_start(out=rows[:, LAST, a:b], in_=res[:, LAST, a:b])
         for q in range(4):
             queue = nc.scalar if q % 2 else nc.sync
             queue.dma_start(
-                out=out_2[0, 4 * q : 4 * q + 4, :].bitcast(I32), in_=out_s[32 * q : 32 * q + 4, :].bitcast(I32)
+                out=out_2[0, 4 * q : 4 * q + 4, :].bitcast(I32), in_=out_scales[32 * q : 32 * q + 4, :].bitcast(I32)
             )

from contextlib import ExitStack

import concourse.mybir as mybir

T, S = 2048, 512
WIDTH = 512
FLOPS = 3 * 2 * 512 * WIDTH * S

F32 = mybir.dt.float32
BF16 = mybir.dt.bfloat16
U32 = mybir.dt.uint32
I32 = mybir.dt.int32
U16 = mybir.dt.uint16
U8 = mybir.dt.uint8
FP8X4 = mybir.dt.float8_e4m3fn_x4
ALU = mybir.AluOpType
ACT = mybir.ActivationFunctionType

P = 128
PACK = 4
HALF = S // 2
HALVES = ((0, HALF), (HALF, S))
LAST = PACK - 1
Y_ON_VECTOR = (2, 3)
H_IN_HALVES = (0, 1)
SPARE = 16


def words_of(dram):
    return dram[0].rearrange("p n t -> p (n t)").bitcast(I32)


def by_rows(column):
    return column.rearrange("(p t) o -> p (t o)", t=PACK)


def load_scale_rows(queue, tile, dram, quadrants):
    for q in quadrants:
        queue.dma_start(
            out=tile[32 * q : 32 * q + 4, :].bitcast(I32),
            in_=dram[0, 4 * q : 4 * q + 4, :].bitcast(I32),
        )


def offsets(lst, a, b):
    return lst[:, a // 16 : b // 16]


def woven(ap):
    return ap.rearrange("p (c i t) -> p c t i", i=4, t=PACK)


def by_fours(ap):
    return ap.rearrange("p t (c i) -> p c t i", i=4)


def tile_picked_twlpxbetw_none_po_kernel(
    tc, x_words, x_scales, w1_words, w1_scales, w2_words, w2_scales, tau, gn, w3_words, w3_scales,
    tau2, tau3, offs, two, n1, n2, n3, n4, out_0, out_1, out_2,
):
    nc = tc.nc
    with ExitStack() as ctx:
        keep = ctx.enter_context(tc.tile_pool(name="keep", bufs=1))
        psum = ctx.enter_context(tc.psum_pool(name="psum", bufs=1))

        def sb(name, shape, dtype, tag=None):
            return keep.tile(shape, dtype, name=name, tag=tag or name, align_bytes=64)

        lists = {nm: keep.tile([P, S // 16], U16, name="list_" + nm) for nm in ("offs", "two", "n1", "n2", "n3", "n4")}
        xw = sb("xw", [P, T], U32)
        xs = sb("xs", [P, T], U8)
        raw_w = {i: sb("raw_w%d" % i, [P, WIDTH], U32) for i in (1, 2, 3)}
        dealt_w = {i: sb("dealt_w%d" % i, [P, WIDTH], U32) for i in (1, 2, 3)}
        raw_s = {i: sb("raw_s%d" % i, [P, WIDTH], U8) for i in (1, 2, 3)}
        dealt_s = {i: sb("dealt_s%d" % i, [P, WIDTH], U8) for i in (1, 2, 3)}
        rate = sb("rate", [P, PACK], F32)
        gain = sb("gain", [P, PACK], F32)
        neg_rate = sb("neg_rate", [P, PACK], F32)
        rate23 = sb("rate23", [P, 2, 8], F32)
        y_sb = [sb("y_sb%d" % t, [P, S + SPARE], F32) for t in range(PACK)]
        h_sb = [sb("h_sb%d" % t, [P, S if t == LAST else 2 * S], F32) for t in range(PACK)]

        nc.vector.memset(xs[:, 0 : T // 2].bitcast(I32), 0)
        nc.gpsimd.memset(xs[:, T // 2 : T].bitcast(I32), 0)
        for i in (2, 1, 3):
            nc.vector.memset(raw_s[i][:].bitcast(I32), 0)
        for t in range(PACK):
            nc.vector.memset(y_sb[t][:, S:], 0.0)

        nc.scalar.dma_start(out=rate[:], in_=by_rows(tau))
        load_scale_rows(nc.scalar, xs, x_scales, (0, 2))
        nc.scalar.dma_start(out=xw[:].bitcast(I32), in_=words_of(x_words))
        nc.scalar.dma_start(out=raw_w[1][:].bitcast(I32), in_=words_of(w1_words))
        nc.scalar.dma_start(out=raw_w[2][:].bitcast(I32), in_=words_of(w2_words))
        nc.scalar.activation(neg_rate[:], rate[:], ACT.Copy, scale=-1.0)
        nc.sync.dma_start(lists["offs"][:], offs)
        nc.sync.dma_start(lists["two"][:], two)
        load_scale_rows(nc.sync, xs, x_scales, (1, 3))
        load_scale_rows(nc.sync, raw_s[1], w1_scales, range(4))
        nc.sync.dma_start(out=raw_w[3][:].bitcast(I32), in_=words_of(w3_words))
        load_scale_rows(nc.sync, raw_s[2], w2_scales, (0,))
        nc.sync.dma_start(lists["n2"][:], n2)
        nc.sync.dma_start(lists["n1"][:], n1)
        nc.sync.dma_start(out=gain[:], in_=by_rows(gn))
        load_scale_rows(nc.sync, raw_s[3], w3_scales, range(4))
        nc.sync.dma_start(lists["n3"][:], n3)
        nc.sync.dma_start(lists["n4"][:], n4)
        for j, column in enumerate((tau2, tau3)):
            nc.sync.dma_start(out=rate23[:, j, 0:PACK], in_=by_rows(column))
        load_scale_rows(nc.gpsimd, raw_s[2], w2_scales, (1, 2, 3))

        def deal_bytes(engine, i):
            engine.tensor_copy(
                out=dealt_s[i][:].rearrange("p (t m) -> p t m", t=PACK),
                in_=raw_s[i][:].rearrange("p (m t) -> p t m", t=PACK),
            )

        def product(bank, i, t, words, scales):
            cols = slice(P * t, P * (t + 1))
            nc.tensor.matmul_mx(
                out=bank, lhsT=dealt_w[i][:, cols].bitcast(FP8X4), lhsT_scale=dealt_s[i][:, cols],
                rhs=words.bitcast(FP8X4), rhs_scale=scales, start=True, stop=True,
            )

        picked_s = {nm: sb("picked_s_" + nm, [P, S], U8) for nm in ("offs", "two")}
        for nm in ("offs", "two"):
            nc.vector.tensor_copy(picked_s[nm][:], xs[:].indirect(lists[nm][:]))
        for i in (1, 2, 3):
            nc.scalar.copy(
                out=dealt_w[i][:].rearrange("p (t m) -> p m t", t=PACK),
                in_=raw_w[i][:].rearrange("p (m t) -> p m t", t=PACK),
            )
        offs_words = sb("offs_words", [P, S], U32)
        nc.vector.tensor_copy(offs_words[:], xw[:].indirect(lists["offs"][:]))
        deal_bytes(nc.vector, 1)
        two_words = sb("two_words", [P, S], U32, tag="raw_s1")
        nc.vector.tensor_copy(two_words[:], xw[:].indirect(lists["two"][:]))
        deal_bytes(nc.vector, 2)

        d_bank = [psum.tile([P, S], F32, name="d_bank%d" % t, tag="d%d" % t) for t in range(PACK)]
        y_bank = [psum.tile([P, S], F32, name="y_bank%d" % t, tag="y%d" % t) for t in range(PACK)]
        for t in range(PACK):
            product(y_bank[t][:], 1, t, offs_words[:], picked_s["offs"][:])
        for t in range(PACK):
            product(d_bank[t][:], 2, t, two_words[:], picked_s["two"][:])

        d_sb = [sb("d_sb%d" % t, [P, S], F32) for t in range(PACK)]
        top = [sb("top%d" % t, [P, 1], F32) for t in range(PACK)]
        bias = [sb("bias%d" % t, [P, 1], F32) for t in range(PACK)]
        for t in Y_ON_VECTOR:
            nc.vector.tensor_scalar(y_sb[t][:, 0:S], y_bank[t][:], 2.0, None, ALU.mult)
        for t in range(PACK):
            nc.vector.tensor_scalar(d_sb[t][:], d_bank[t][:], 1.0, None, ALU.mult, ALU.max, accum_out=top[t][:])
            nc.vector.tensor_scalar(bias[t][:], top[t][:], neg_rate[:, t : t + 1], None, ALU.mult)

        y_got = sb("y_got", [P, PACK, S], F32)
        for t in range(PACK):
            if t not in Y_ON_VECTOR:
                nc.scalar.activation(y_sb[t][:, 0:S], y_bank[t][:], ACT.Copy, scale=2.0)
            nc.scalar.activation(y_got[:, t, :], y_sb[t][:].indirect(lists["n2"][:]), ACT.Copy)

        d_half = sb("d_half", [P, PACK, S], F32)
        for t in range(PACK):
            nc.gpsimd.tensor_scalar(d_half[:, t, :], d_sb[t][:], gain[:, t : t + 1], -0.5, ALU.mult, ALU.mult)

        def fetch_ea(k, tag):
            a, b = HALVES[k]
            ea = sb("ea%d" % k, [P, PACK, HALF], F32, tag)
            for t in range(PACK):
                nc.scalar.activation(
                    ea[:, t, :], d_sb[t][:].indirect(offsets(lists["n1"], a, b)), ACT.Exp,
                    bias=bias[t][:], scale=rate[:, t : t + 1],
                )
            return ea

        def make_z(k, ea):
            a, b = HALVES[k]
            pull = sb("pull%d" % k, [P, PACK, HALF], F32, tag="pull")
            z = sb("z%d" % k, [P, PACK * HALF], BF16)
            words = sb("z_words%d" % k, [P, HALF], U32)
            scales = sb("z_scales%d" % k, [P, HALF], U8)
            for t in range(PACK):
                nc.vector.scalar_tensor_tensor(
                    pull[:, t, :], gap[t][:, a:b], gain[:, t : t + 1], ea[:, t, :], ALU.mult, ALU.mult
                )
            nc.vector.tensor_tensor(woven(z[:]), by_fours(pull[:]), by_fours(d_half[:, :, a:b]), ALU.add)
            nc.vector.quantize_mx(out=words[:].bitcast(FP8X4), scales=scales[:], in_=z[:])
            return words, scales

        ea_low = fetch_ea(0, None)
        deal_bytes(nc.gpsimd, 3)
        neg_rate23 = sb("neg_rate23", [P, 2, PACK], F32)
        nc.gpsimd.tensor_scalar(neg_rate23[:], rate23[:, :, 0:PACK], -1.0, 0.0, ALU.mult, ALU.add)
        gap = [sb("gap_last", [P, S], F32)[:] if t == LAST else h_sb[t][:, S:] for t in range(PACK)]
        for t in range(PACK):
            nc.vector.scalar_tensor_tensor(gap[t], y_bank[t][:], 2.0, y_got[:, t, :], ALU.mult, ALU.subtract)
        z_low = make_z(0, ea_low)
        ea_high = fetch_ea(1, "top%d" % LAST)
        z_high = make_z(1, ea_high)

        h_low = [psum.tile([P, S], F32, name="h_low%d" % t, tag="d%d" % t) for t in range(PACK)]
        h_high = [
            psum.tile([P, S], F32, name="h_high%d" % t, tag="y%d" % t) if t in H_IN_HALVES else h_low[t]
            for t in range(PACK)
        ]
        for t in range(PACK):
            product(h_low[t][:, 0:HALF], 3, t, z_low[0][:], z_low[1][:])
        for t in range(PACK):
            product(h_high[t][:, HALF:S], 3, t, z_high[0][:], z_high[1][:])

        top_low = [sb("top_low%d" % t, [P, 1], F32, tag) for t, tag in zip(H_IN_HALVES, ("pull", "d_half"))]
        top2 = [sb("top2_%d" % t, [P, 1], F32) for t in range(PACK)]
        bias23 = [sb("bias23_%d" % t, [P, 2], F32) for t in range(PACK)]
        for t in range(PACK):
            if t in H_IN_HALVES:
                nc.vector.tensor_scalar(
                    h_sb[t][:, 0:HALF], h_low[t][:, 0:HALF], 1.0, None, ALU.mult, ALU.max, accum_out=top_low[t][:]
                )
                nc.vector.tensor_scalar(
                    h_sb[t][:, HALF:S], h_high[t][:, HALF:S], 1.0, top_low[t][:], ALU.mult, ALU.max,
                    accum_out=top2[t][:],
                )
            else:
                nc.vector.tensor_scalar(h_sb[t][:, 0:S], h_low[t][:], 1.0, None, ALU.mult, ALU.max, accum_out=top2[t][:])
            if t == 0:
                nc.scalar.activation(bias23[t][:], neg_rate23[:, :, t], ACT.Copy, scale=top2[t][:])
            else:
                nc.vector.tensor_scalar(bias23[t][:], neg_rate23[:, :, t], top2[t][:], None, ALU.mult)

        out_words = sb("out_words", [P, S], U32)
        out_scales = sb("out_scales", [P, S], U8)
        ea2 = sb("ea2", [P, PACK, S], F32)
        ea3 = sb("ea3", [P, PACK, S], F32)
        diff = sb("diff", [P, PACK, S], F32)
        res = sb("res", [P, PACK, S], F32)
        rows = out_0.rearrange("(p t) j -> p t j", t=PACK)

        def make_diff(t, a, b):
            for got, lst, j in ((ea2, "n3", 0), (ea3, "n4", 1)):
                nc.scalar.activation(
                    got[:, t, a:b], h_sb[t][:].indirect(offsets(lists[lst], a, b)), ACT.Exp,
                    bias=bias23[t][:, j : j + 1], scale=rate23[:, j, t : t + 1],
                )
            nc.vector.tensor_tensor(diff[:, t, a:b], ea2[:, t, a:b], ea3[:, t, a:b], ALU.subtract)

        for t in range(LAST):
            make_diff(t, 0, S)
            nc.vector.tensor_scalar(res[:, t, :], diff[:, t, :], 3.0, None, ALU.mult)
            nc.sync.dma_start(out=rows[:, t, :], in_=res[:, t, :])
        for k, (a, b) in enumerate(HALVES):
            make_diff(LAST, a, b)
            rounded = sb("rounded%d" % k, [P, PACK * HALF], BF16)
            nc.vector.tensor_scalar(woven(rounded[:]), by_fours(diff[:, :, a:b]), 3.0, None, ALU.mult)
            nc.vector.quantize_mx(out=out_words[:, a:b].bitcast(FP8X4), scales=out_scales[:, a:b], in_=rounded[:])
            nc.sync.dma_start(out=words_of(out_1)[:, a:b], in_=out_words[:, a:b].bitcast(I32))
            if b == S:
                nc.scalar.activation(res[:, LAST, a:b], diff[:, LAST, a:b], ACT.Copy, scale=3.0)
            else:
                nc.vector.tensor_scalar(res[:, LAST, a:b], diff[:, LAST, a:b], 3.0, None, ALU.mult)
            nc.sync.dma_start(out=rows[:, LAST, a:b], in_=res[:, LAST, a:b])
        for q in range(4):
            queue = nc.scalar if q % 2 else nc.sync
            queue.dma_start(
                out=out_2[0, 4 * q : 4 * q + 4, :].bitcast(I32), in_=out_scales[32 * q : 32 * q + 4, :].bitcast(I32)
            )
